import numpy as np
import ml_dtypes


def mxq(x, axis, fmt="e4m3"):
    dtype, down = {"e4m3": (ml_dtypes.float8_e4m3fn, 7), "e5m2": (ml_dtypes.float8_e5m2, 14)}[fmt]
    v = np.moveaxis(np.asarray(x, np.float32).astype(ml_dtypes.bfloat16).astype(np.float64), axis, -1)
    blocks = v.reshape(v.shape[:-1] + (-1, 32))
    amax = np.abs(blocks).max(-1, keepdims=True)
    byte = np.maximum(np.where(amax > 0, np.frexp(amax)[1] - 1 + 127, 0) - down, 1)
    scale = np.exp2(byte - 127.0)
    codes = (blocks / scale).astype(np.float32).astype(dtype).astype(np.float64)
    return np.moveaxis((codes * scale).reshape(v.shape), -1, axis)


WIDE = False


def mx_kscale(k):
    if not WIDE:
        return np.ones(k)
    levels = np.array([10, -10, 5, -5, 0])
    if k % 512:
        return np.exp2(np.random.permutation(np.resize(levels, k // 32))).repeat(32)
    a = np.empty((k // 512, 16))
    for p in range(k // 512):
        a[p, :8] = np.random.permutation(np.resize(levels, 8))
        for g in range(8):
            far = levels[np.abs(levels - a[p, g]) >= 10]
            a[p, g + 8] = far[np.random.randint(len(far))]
    return np.exp2(a.ravel()).repeat(32)


def f64(x):
    return np.asarray(x).astype(np.float64)


def striped(idx):
    return np.tile(idx.reshape(-1, 16).T, (8, 1)).astype(np.uint16)


def unstriped(offs):
    return offs[:16].T.reshape(-1).astype(np.int64)


def pack_weight(w):
    k, n = w.shape
    w = f64(np.asarray(w, np.float32).astype(ml_dtypes.bfloat16)).reshape(k // 32, 32, n)
    amax = np.abs(w).max(1)
    byte = np.clip(np.where(amax > 0, np.frexp(amax)[1] - 1 + 127 - 7, 1), 1, 254)
    scaled = (w * np.exp2(127.0 - byte)[:, None, :]).reshape(k, n).astype(np.float32)
    words = np.ascontiguousarray(scaled.reshape(k // 512, 128, 4, n).transpose(0, 1, 3, 2)).astype(ml_dtypes.float8_e4m3fn).view(np.uint8)
    return words, np.ascontiguousarray(byte.astype(np.uint8).reshape(k // 512, 16, n))


def unpack_weight(words, scales):
    g, p, n, _ = words.shape
    vals = np.ascontiguousarray(words).view(ml_dtypes.float8_e4m3fn).astype(np.float64) * np.repeat(np.exp2(scales.astype(np.float64) - 127.0), 8, axis=1)[..., None]
    return vals.transpose(0, 1, 3, 2).reshape(g * 512, n)


E2M1 = np.array([0.0, 0.5, 1.0, 1.5, 2.0, 3.0, 4.0, 6.0, -0.0, -0.5, -1.0, -1.5, -2.0, -3.0, -4.0, -6.0])


def pack_fp4(w):
    k, n = w.shape
    w = f64(np.asarray(w, np.float32).astype(ml_dtypes.bfloat16)).reshape(k // 32, 32, n)
    amax = np.abs(w).max(1)
    mant, ex = np.frexp(amax / 6.0)
    byte = np.clip(np.where(amax > 0, np.where(mant > 0.5, ex, ex - 1) + 127, 1), 1, 254)
    scaled = (w * np.exp2(127.0 - byte)[:, None, :]).reshape(k, n).astype(np.float32)
    c = np.ascontiguousarray(scaled.reshape(k // 512, 128, 4, n).transpose(0, 1, 3, 2)).astype(ml_dtypes.float4_e2m1fn).view(np.uint8) & 0xF
    words = (c[..., 0::2] | (c[..., 1::2] << 4)).reshape(k // 512, 128, 2 * n)
    return np.ascontiguousarray(words), np.ascontiguousarray(byte.astype(np.uint8).reshape(k // 512, 16, n))


def unpack_fp4(words, scales):
    g, _, n = scales.shape
    words = np.ascontiguousarray(words).reshape(g, 128, n, 2)
    nib = np.empty((g, 128, n, 4), np.uint8)
    nib[..., 0::2] = words & 0xF
    nib[..., 1::2] = words >> 4
    vals = E2M1[nib] * np.repeat(np.exp2(scales.astype(np.float64) - 127.0), 8, axis=1)[..., None]
    return vals.transpose(0, 1, 3, 2).reshape(g * 512, n)


K, T, S, N, H, U = 512, 1024, 512, 128, 512, 1024


def setup_inputs():
    n = np.random.standard_normal
    s = mx_kscale(K)[:, None]
    u = mx_kscale(H)
    packed_xT = pack_weight(n((K, T)) * s)
    packed_w1 = pack_fp4(n((K, H)) / np.sqrt(K) / s)
    packed_w2 = pack_fp4(n((K, H)) / np.sqrt(K) / s)
    packed_w3 = pack_fp4(n((H, N)) / np.sqrt(H) / u[:, None])
    return {
        "x_words": packed_xT[0],
        "x_scales": packed_xT[1],
        "w1_words": packed_w1[0],
        "w1_scales": packed_w1[1],
        "w2_words": packed_w2[0],
        "w2_scales": packed_w2[1],
        "rad": (np.random.uniform(0.6, 2.5, (H, U))).astype(np.float32),
        "unit": (np.random.uniform(0.6, 1.4, (H, 1)) * u[:, None]).astype(np.float32),
        "w3_words": packed_w3[0],
        "w3_scales": packed_w3[1],
        "offs": striped(np.random.permutation(T)[:S]),
        "pa": striped(np.random.permutation(np.concatenate([np.arange(S), np.random.randint(0, S, U - S)]))),
        "pb": striped(np.random.permutation(np.concatenate([np.arange(S), np.random.randint(0, S, U - S)]))),
    }


def reference(x_words, x_scales, w1_words, w1_scales, w2_words, w2_scales, rad, unit, w3_words, w3_scales, offs, pa, pb):
    xq = unpack_weight(x_words, x_scales)[:, unstriped(offs)]
    ure = unpack_fp4(w1_words, w1_scales).T @ xq
    ra = ure[:, unstriped(pa)]
    ga = ra / f64(rad)
    uim = unpack_fp4(w2_words, w2_scales).T @ xq
    ib = uim[:, unstriped(pb)]
    gb = ib / (f64(rad) + 0.5)
    pr2 = (ga) ** 2 + (gb) ** 2 + 0.8 * (ga * gb)
    ampl = np.sqrt(pr2 + 0.05)
    ia = uim[:, unstriped(pa)]
    hid = f64(unit) * (np.log(ampl + 0.2) * ia)
    return unpack_fp4(w3_words, w3_scales).T @ mxq(hid, 0, "e4m3")

@@ -1,0 +1,224 @@
+import math
+from contextlib import ExitStack
+
+import concourse.mybir as mybir
+from concourse.masks import make_identity
+
+K, T, S, N, H, U = 512, 1024, 512, 128, 512, 1024
+FLOPS = 2 * K * S * H * 2 + 2 * H * U * N
+
+F32 = mybir.dt.float32
+BF16 = mybir.dt.bfloat16
+I32 = mybir.dt.int32
+U32 = mybir.dt.uint32
+U16 = mybir.dt.uint16
+U8 = mybir.dt.uint8
+FP8X4 = mybir.dt.float8_e4m3fn_x4
+FP4X4 = mybir.dt.float4_e2m1fn_x4
+ACT = mybir.ActivationFunctionType
+ALU = mybir.AluOpType
+
+P = 128
+PACK = 4
+BANK = 512
+SPARE = 16
+GROUP = 256
+
+
+def load_scale_rows(queue, tile, scales):
+    for q in range(4):
+        queue.dma_start(out=tile[32 * q : 32 * q + 4, :].bitcast(I32), in_=scales[0, 4 * q : 4 * q + 4, :].bitcast(I32))
+
+
+def tile_picked_yacoust_log_p_kernel(
+    tc, x_words, x_scales, w1_words, w1_scales, w2_words, w2_scales, rad, unit, w3_words, w3_scales, offs, pa, pb, out
+):
+    nc = tc.nc
+    with ExitStack() as ctx:
+        keep = ctx.enter_context(tc.tile_pool(name="keep", bufs=1))
+        ring = ctx.enter_context(tc.tile_pool(name="ring", bufs=2))
+        psum = ctx.enter_context(tc.psum_pool(name="psum", bufs=1))
+
+        def bank(b):
+            return psum.tile([P, BANK], F32, name=f"bank{b}", tag=f"bank{b}")
+
+        offs_t = keep.tile([P, S // 16], U16, name="offs_t")
+        pa_t = keep.tile([P, U // 16], U16, name="pa_t")
+        pb_t = keep.tile([P, U // 16], U16, name="pb_t")
+        xw = keep.tile([P, T], I32, name="xw", align_bytes=64)
+        xs = keep.tile([P, T], U8, name="xs", align_bytes=64)
+        ww = [keep.tile([P, 2 * H], U8, name=f"ww{i}", align_bytes=64) for i in range(2)]
+        ws = [keep.tile([P, H], U8, name=f"ws{i}", align_bytes=64) for i in range(2)]
+        w3w = keep.tile([P, 2 * N], U8, name="w3w", align_bytes=64)
+        w3s = keep.tile([P, N], U8, name="w3s", align_bytes=64)
+        unit_t = keep.tile([P, PACK], F32, name="unit_t")
+        rad_t = [keep.tile([P, U], F32, name=f"rad{t}", align_bytes=64) for t in range(PACK)]
+        rad_rows = rad.rearrange("(p t) r -> p t r", t=PACK)
+
+        for tile in (xs, ws[0]):
+            nc.gpsimd.memset(tile[:].bitcast(I32), 0)
+        for tile in (ws[1], w3s):
+            nc.vector.memset(tile[:].bitcast(I32), 0)
+
+        nc.sync.dma_start(offs_t[:], offs)
+        nc.sync.dma_start(out=xw[:], in_=x_words[0].rearrange("p n t -> p (n t)").bitcast(I32))
+        nc.scalar.dma_start(out=rad_t[0][:], in_=rad_rows[:, 0, :])
+        nc.scalar.dma_start(out=ww[0][:].bitcast(I32), in_=w1_words[0].bitcast(I32))
+        load_scale_rows(nc.sync, xs, x_scales)
+        load_scale_rows(nc.gpsimd, ws[1], w2_scales)
+        load_scale_rows(nc.sync, ws[0], w1_scales)
+        nc.sync.dma_start(out=ww[1][:].bitcast(I32), in_=w2_words[0].bitcast(I32))
+        nc.sync.dma_start(out=rad_t[1][:], in_=rad_rows[:, 1, :])
+        nc.sync.dma_start(pa_t[:], pa)
+        nc.sync.dma_start(pb_t[:], pb)
+        nc.gpsimd.dma_start(out=unit_t[:], in_=unit.rearrange("(p t) o -> p (t o)", t=PACK))
+        nc.sync.dma_start(out=rad_t[2][:], in_=rad_rows[:, 2, :])
+        nc.sync.dma_start(out=rad_t[3][:], in_=rad_rows[:, 3, :])
+        nc.sync.dma_start(out=w3w[:].bitcast(I32), in_=w3_words[0].bitcast(I32))
+        load_scale_rows(nc.sync, w3s, w3_scales)
+
+        ure = [keep.tile([P, S + SPARE], F32, name=f"ure{t}", align_bytes=64) for t in range(PACK)]
+        uim = [keep.tile([P, S + SPARE], F32, name=f"uim{t}", align_bytes=64) for t in range(PACK)]
+        uimu = [keep.tile([P, S + SPARE], F32, name=f"uimu{t}", align_bytes=64) for t in range(PACK)]
+        for tile in ure + uim + uimu:
+            nc.gpsimd.memset(tile[:, S:], 0.0)
+        ident = keep.tile([P, P], F32, name="ident", align_bytes=64)
+        make_identity(nc, ident[:])
+
+        xgw = keep.tile([P, S], U32, name="xgw", align_bytes=64)
+        xgs = keep.tile([P, S], U8, name="xgs", align_bytes=64)
+        wd = [keep.tile([P, 2 * H], U8, name=f"wd{i}", align_bytes=64) for i in range(2)]
+        wsd = [keep.tile([P, H], U8, name=f"wsd{i}", align_bytes=64) for i in range(2)]
+
+        def deal_words(i):
+            nc.vector.tensor_copy(
+                out=wd[i][:].rearrange("p (t m b) -> p t m b", t=PACK, b=2),
+                in_=ww[i][:].rearrange("p (m t b) -> p t m b", t=PACK, b=2),
+            )
+
+        def deal_scales(i):
+            nc.vector.tensor_copy(
+                out=wsd[i][:].rearrange("p (t m) -> p t m", t=PACK),
+                in_=ws[i][:].rearrange("p (m t) -> p t m", t=PACK),
+            )
+
+        nc.vector.tensor_copy(xgw[:], xw[:].bitcast(U32).indirect(offs_t[:]))
+        nc.vector.tensor_copy(xgs[:], xs[:].indirect(offs_t[:]))
+        deal_words(0)
+        deal_scales(0)
+        deal_words(1)
+        deal_scales(1)
+
+        def product(i, t):
+            acc = bank(2 * t + i)
+            nc.tensor.matmul_mx(
+                out=acc[:],
+                lhsT=wd[i][:, 2 * P * t : 2 * P * (t + 1)].bitcast(FP4X4),
+                lhsT_scale=wsd[i][:, P * t : P * (t + 1)],
+                rhs=xgw[:].bitcast(FP8X4),
+                rhs_scale=xgs[:],
+                start=True,
+                stop=True,
+            )
+            return acc
+
+        lnr = keep.tile([P, PACK, U], F32, name="lnr", tag="lnr", align_bytes=64)
+        inv_a = keep.tile([P, PACK, U], F32, name="inv_a", align_bytes=64)
+        for t in range(PACK):
+            nc.scalar.activation(lnr[:, t, :], rad_t[t][:], ACT.Ln, scale=2.0)
+        for t in range(PACK):
+            nc.vector.tensor_copy(ure[t][:, :S], product(0, t)[:])
+            nc.vector.tensor_copy(uim[t][:, :S], product(1, t)[:])
+        for t in range(PACK):
+            nc.vector.tensor_scalar(uimu[t][:, :S], uim[t][:, :S], unit_t[:, t : t + 1], None, ALU.mult)
+        halves = range(U // BANK)
+        for h in halves:
+            cols = slice(BANK * h, BANK * (h + 1))
+            nc.scalar.activation(inv_a[:, :, cols], lnr[:, :, cols], ACT.Exp, scale=-1.0, bias=math.log(2.5))
+        for t in range(PACK):
+            nc.scalar.activation(lnr[:, t, :], lnr[:, t, :], ACT.Sigmoid, scale=-1.0)
+
+        def piece(tile, h):
+            return tile[:, BANK // 16 * h : BANK // 16 * (h + 1)]
+
+        ga = {}
+
+        for h in halves:
+            for t in range(PACK):
+                cols = slice(BANK * h, BANK * (h + 1))
+                ga[t, h] = keep.tile([P, BANK], F32, name=f"ga{t}{h}", tag=f"ga{t}{h}", align_bytes=64)
+                nc.vector.tensor_tensor(ga[t, h][:], ure[t][:].indirect(piece(pa_t, h)), inv_a[:, t, cols], ALU.mult)
+
+        amp = keep.tile([P, PACK, U], F32, name="amp", align_bytes=64)
+        blocks = BANK // P
+        for t in range(PACK):
+            sq_sum = ring.tile([P, U // P, P], F32, name="sq_sum", align_bytes=64)
+            sq_b = ring.tile([P, U // P, P], F32, name="sq_b", align_bytes=64)
+            for h in halves:
+                cols = slice(BANK * h, BANK * (h + 1))
+                gb = ring.tile([P, BANK], F32, name="gb", align_bytes=64, bufs=8)
+                nc.vector.tensor_tensor(gb[:], uim[t][:].indirect(piece(pb_t, h)), lnr[:, t, cols], ALU.mult)
+                both, alone = bank(2 * h), bank(2 * h + 1)
+                for j in range(blocks):
+                    blk = slice(P * j, P * (j + 1))
+                    nc.tensor.transpose(alone[:, blk], gb[:, blk], ident[:])
+                for j in range(blocks):
+                    blk = slice(P * j, P * (j + 1))
+                    nc.tensor.matmul(both[:, blk], ga[t, h][:, blk], ident[:], start=True, stop=False, is_transpose=True)
+                    nc.tensor.matmul(both[:, blk], gb[:, blk], ident[:], start=False, stop=True, is_transpose=True)
+                dst = slice(blocks * h, blocks * (h + 1))
+                nc.scalar.activation(
+                    sq_b[:, dst, :], alone[:].rearrange("p (j f) -> p j f", f=P), ACT.Square, scale=math.sqrt(3.36)
+                )
+                nc.scalar.activation(sq_sum[:, dst, :], both[:].rearrange("p (j f) -> p j f", f=P), ACT.Square, scale=0.8)
+            for h in range(2):
+                total = bank(4 + 2 * (t % 2) + h)
+                for j in range(blocks):
+                    blk = slice(P * j, P * (j + 1))
+                    src = 2 * j + h
+                    nc.tensor.matmul(total[:, blk], sq_b[:, src, :], ident[:], start=True, stop=False, is_transpose=True)
+                    nc.tensor.matmul(total[:, blk], sq_sum[:, src, :], ident[:], start=False, stop=True, is_transpose=True)
+                nc.scalar.activation(
+                    amp[:, t, :].rearrange("p (j h r) -> p j h r", h=2, r=P)[:, :, h, :],
+                    total[:].rearrange("p (j r) -> p j r", r=P),
+                    ACT.Sqrt,
+                    bias=0.05,
+                )
+
+        ia_early = keep.tile([P, PACK, GROUP], F32, name="ia_early", align_bytes=64)
+        ia_late = keep.tile([P, PACK, U], F32, name="ia_late", tag="lnr", align_bytes=64)
+        for t in range(PACK):
+            nc.vector.tensor_copy(ia_early[:, t, :], uimu[t][:].indirect(pa_t[:, : GROUP // 16]))
+        for lo, hi in ((GROUP, BANK), (BANK, U)):
+            for t in range(PACK):
+                nc.vector.tensor_copy(ia_late[:, t, lo:hi], uimu[t][:].indirect(pa_t[:, lo // 16 : hi // 16]))
+
+        for g in range(U // GROUP):
+            cols = slice(GROUP * g, GROUP * (g + 1))
+            lg = ring.tile([P, PACK, GROUP], F32, name="lg", align_bytes=64, bufs=4)
+            nc.scalar.activation(lg[:], amp[:, :, cols], ACT.Ln, bias=0.2)
+            woven = ring.tile([P, GROUP, PACK], BF16, name="woven", align_bytes=64)
+            nc.vector.tensor_tensor(
+                woven[:].rearrange("p (c i) t -> p c t i", i=2),
+                (ia_early[:] if g == 0 else ia_late[:, :, cols]).rearrange("p t (c i) -> p c t i", i=2),
+                lg[:].rearrange("p t (c i) -> p c t i", i=2),
+                ALU.mult,
+            )
+            codes = ring.tile([P, GROUP], U32, name="codes", align_bytes=64)
+            scales = ring.tile([P, GROUP], U8, name="scales", align_bytes=64)
+            nc.vector.quantize_mx(
+                out=codes[:].bitcast(FP8X4), scales=scales[:], in_=woven[:].rearrange("p n t -> p (n t)")
+            )
+            acc = bank(g)
+            nc.tensor.matmul_mx(
+                out=acc[:, :GROUP],
+                lhsT=w3w[:].bitcast(FP4X4),
+                lhsT_scale=w3s[:],
+                rhs=codes[:].bitcast(FP8X4),
+                rhs_scale=scales[:],
+                start=True,
+                stop=True,
+            )
+            res = ring.tile([P, GROUP], F32, name="res", align_bytes=64, bufs=4)
+            nc.scalar.copy(res[:], acc[:, :GROUP])
+            nc.sync.dma_start(out=out[:, cols], in_=res[:])

@@ -23,6 +23,7 @@ PACK = 4
 BANK = 512
 SPARE = 16
 GROUP = 256
+SHIFT = 41.5
 
 
 def load_scale_rows(queue, tile, scales):
@@ -52,28 +53,26 @@ def tile_picked_yacoust_log_p_kernel(
         w3w = keep.tile([P, 2 * N], U8, name="w3w", align_bytes=64)
         w3s = keep.tile([P, N], U8, name="w3s", align_bytes=64)
         unit_t = keep.tile([P, PACK], F32, name="unit_t")
-        rad_t = [keep.tile([P, U], F32, name=f"rad{t}", align_bytes=64) for t in range(PACK)]
+        rad_t = [keep.tile([P, PACK, GROUP], F32, name=f"rad{g}", align_bytes=64) for g in range(U // GROUP)]
         rad_rows = rad.rearrange("(p t) r -> p t r", t=PACK)
 
-        for tile in (xs, ws[0]):
+        for tile in (xs, ws[0], ws[1], w3s):
             nc.gpsimd.memset(tile[:].bitcast(I32), 0)
-        for tile in (ws[1], w3s):
-            nc.vector.memset(tile[:].bitcast(I32), 0)
 
-        nc.sync.dma_start(offs_t[:], offs)
         nc.sync.dma_start(out=xw[:], in_=x_words[0].rearrange("p n t -> p (n t)").bitcast(I32))
-        nc.scalar.dma_start(out=rad_t[0][:], in_=rad_rows[:, 0, :])
+        nc.sync.dma_start(offs_t[:], offs)
+        nc.scalar.dma_start(out=rad_t[0][:], in_=rad_rows[:, :, 0 * GROUP : 1 * GROUP])
         nc.scalar.dma_start(out=ww[0][:].bitcast(I32), in_=w1_words[0].bitcast(I32))
         load_scale_rows(nc.sync, xs, x_scales)
-        load_scale_rows(nc.gpsimd, ws[1], w2_scales)
+        nc.sync.dma_start(out=rad_t[1][:], in_=rad_rows[:, :, 1 * GROUP : 2 * GROUP])
         load_scale_rows(nc.sync, ws[0], w1_scales)
+        nc.sync.dma_start(out=rad_t[2][:], in_=rad_rows[:, :, 2 * GROUP : 3 * GROUP])
+        nc.sync.dma_start(out=rad_t[3][:], in_=rad_rows[:, :, 3 * GROUP : 4 * GROUP])
         nc.sync.dma_start(out=ww[1][:].bitcast(I32), in_=w2_words[0].bitcast(I32))
-        nc.sync.dma_start(out=rad_t[1][:], in_=rad_rows[:, 1, :])
+        load_scale_rows(nc.sync, ws[1], w2_scales)
+        nc.sync.dma_start(out=unit_t[:], in_=unit.rearrange("(p t) o -> p (t o)", t=PACK))
         nc.sync.dma_start(pa_t[:], pa)
         nc.sync.dma_start(pb_t[:], pb)
-        nc.gpsimd.dma_start(out=unit_t[:], in_=unit.rearrange("(p t) o -> p (t o)", t=PACK))
-        nc.sync.dma_start(out=rad_t[2][:], in_=rad_rows[:, 2, :])
-        nc.sync.dma_start(out=rad_t[3][:], in_=rad_rows[:, 3, :])
         nc.sync.dma_start(out=w3w[:].bitcast(I32), in_=w3_words[0].bitcast(I32))
         load_scale_rows(nc.sync, w3s, w3_scales)
 
@@ -124,30 +123,19 @@ def tile_picked_yacoust_log_p_kernel(
 
         lnr = keep.tile([P, PACK, U], F32, name="lnr", tag="lnr", align_bytes=64)
         inv_a = keep.tile([P, PACK, U], F32, name="inv_a", align_bytes=64)
+        for g in range(U // GROUP):
+            nc.scalar.activation(lnr[:, :, GROUP * g : GROUP * (g + 1)], rad_t[g][:], ACT.Ln, scale=2.0)
         for t in range(PACK):
-            nc.scalar.activation(lnr[:, t, :], rad_t[t][:], ACT.Ln, scale=2.0)
+            nc.vector.tensor_scalar(ure[t][:, :S], product(0, t)[:], 2.5 * math.exp(SHIFT), None, ALU.mult)
         for t in range(PACK):
-            nc.vector.tensor_copy(ure[t][:, :S], product(0, t)[:])
             nc.vector.tensor_copy(uim[t][:, :S], product(1, t)[:])
-        for t in range(PACK):
-            nc.vector.tensor_scalar(uimu[t][:, :S], uim[t][:, :S], unit_t[:, t : t + 1], None, ALU.mult)
         halves = range(U // BANK)
-        for h in halves:
-            cols = slice(BANK * h, BANK * (h + 1))
-            nc.scalar.activation(inv_a[:, :, cols], lnr[:, :, cols], ACT.Exp, scale=-1.0, bias=math.log(2.5))
         for t in range(PACK):
+            nc.scalar.activation(inv_a[:, t, :], lnr[:, t, :], ACT.Sigmoid, scale=-1.0, bias=-SHIFT)
             nc.scalar.activation(lnr[:, t, :], lnr[:, t, :], ACT.Sigmoid, scale=-1.0)
 
         def piece(tile, h):
             return tile[:, BANK // 16 * h : BANK // 16 * (h + 1)]
-
-        ga = {}
-
-        for h in halves:
-            for t in range(PACK):
-                cols = slice(BANK * h, BANK * (h + 1))
-                ga[t, h] = keep.tile([P, BANK], F32, name=f"ga{t}{h}", tag=f"ga{t}{h}", align_bytes=64)
-                nc.vector.tensor_tensor(ga[t, h][:], ure[t][:].indirect(piece(pa_t, h)), inv_a[:, t, cols], ALU.mult)
 
         amp = keep.tile([P, PACK, U], F32, name="amp", align_bytes=64)
         blocks = BANK // P
@@ -156,7 +144,9 @@ def tile_picked_yacoust_log_p_kernel(
             sq_b = ring.tile([P, U // P, P], F32, name="sq_b", align_bytes=64)
             for h in halves:
                 cols = slice(BANK * h, BANK * (h + 1))
+                ga = ring.tile([P, BANK], F32, name="ga", align_bytes=64, bufs=8)
                 gb = ring.tile([P, BANK], F32, name="gb", align_bytes=64, bufs=8)
+                nc.vector.tensor_tensor(ga[:], ure[t][:].indirect(piece(pa_t, h)), inv_a[:, t, cols], ALU.mult)
                 nc.vector.tensor_tensor(gb[:], uim[t][:].indirect(piece(pb_t, h)), lnr[:, t, cols], ALU.mult)
                 both, alone = bank(2 * h), bank(2 * h + 1)
                 for j in range(blocks):
@@ -164,13 +154,16 @@ def tile_picked_yacoust_log_p_kernel(
                     nc.tensor.transpose(alone[:, blk], gb[:, blk], ident[:])
                 for j in range(blocks):
                     blk = slice(P * j, P * (j + 1))
-                    nc.tensor.matmul(both[:, blk], ga[t, h][:, blk], ident[:], start=True, stop=False, is_transpose=True)
+                    nc.tensor.matmul(both[:, blk], ga[:, blk], ident[:], start=True, stop=False, is_transpose=True)
                     nc.tensor.matmul(both[:, blk], gb[:, blk], ident[:], start=False, stop=True, is_transpose=True)
                 dst = slice(blocks * h, blocks * (h + 1))
                 nc.scalar.activation(
                     sq_b[:, dst, :], alone[:].rearrange("p (j f) -> p j f", f=P), ACT.Square, scale=math.sqrt(3.36)
                 )
                 nc.scalar.activation(sq_sum[:, dst, :], both[:].rearrange("p (j f) -> p j f", f=P), ACT.Square, scale=0.8)
+            if t == 0:
+                for u in range(PACK):
+                    nc.vector.tensor_scalar(uimu[u][:, :S], uim[u][:, :S], unit_t[:, u : u + 1], None, ALU.mult)
             for h in range(2):
                 total = bank(4 + 2 * (t % 2) + h)
                 for j in range(blocks):
@@ -186,9 +179,9 @@ def tile_picked_yacoust_log_p_kernel(
                 )
 
         ia_early = keep.tile([P, PACK, GROUP], F32, name="ia_early", align_bytes=64)
-        ia_late = keep.tile([P, PACK, U], F32, name="ia_late", tag="lnr", align_bytes=64)
         for t in range(PACK):
-            nc.vector.tensor_copy(ia_early[:, t, :], uimu[t][:].indirect(pa_t[:, : GROUP // 16]))
+            nc.scalar.activation(ia_early[:, t, :], uimu[t][:].indirect(pa_t[:, : GROUP // 16]), ACT.Copy)
+        ia_late = keep.tile([P, PACK, U], F32, name="ia_late", tag="lnr", align_bytes=64)
         for lo, hi in ((GROUP, BANK), (BANK, U)):
             for t in range(PACK):
                 nc.vector.tensor_copy(ia_late[:, t, lo:hi], uimu[t][:].indirect(pa_t[:, lo // 16 : hi // 16]))

@@ -62,9 +62,9 @@ def tile_picked_yacoust_log_p_kernel(
         nc.sync.dma_start(out=xw[:], in_=x_words[0].rearrange("p n t -> p (n t)").bitcast(I32))
         nc.sync.dma_start(offs_t[:], offs)
         nc.scalar.dma_start(out=rad_t[0][:], in_=rad_rows[:, :, 0 * GROUP : 1 * GROUP])
-        nc.scalar.dma_start(out=ww[0][:].bitcast(I32), in_=w1_words[0].bitcast(I32))
+        nc.scalar.dma_start(out=rad_t[1][:], in_=rad_rows[:, :, 1 * GROUP : 2 * GROUP])
         load_scale_rows(nc.sync, xs, x_scales)
-        nc.sync.dma_start(out=rad_t[1][:], in_=rad_rows[:, :, 1 * GROUP : 2 * GROUP])
+        nc.sync.dma_start(out=ww[0][:].bitcast(I32), in_=w1_words[0].bitcast(I32))
         load_scale_rows(nc.sync, ws[0], w1_scales)
         nc.sync.dma_start(out=rad_t[2][:], in_=rad_rows[:, :, 2 * GROUP : 3 * GROUP])
         nc.sync.dma_start(out=rad_t[3][:], in_=rad_rows[:, :, 3 * GROUP : 4 * GROUP])
@@ -78,7 +78,7 @@ def tile_picked_yacoust_log_p_kernel(
 
         ure = [keep.tile([P, S + SPARE], F32, name=f"ure{t}", align_bytes=64) for t in range(PACK)]
         uim = [keep.tile([P, S + SPARE], F32, name=f"uim{t}", align_bytes=64) for t in range(PACK)]
-        uimu = [keep.tile([P, S + SPARE], F32, name=f"uimu{t}", align_bytes=64) for t in range(PACK)]
+        uimu = [keep.tile([P, U - GROUP + SPARE], F32, name=f"uimu{t}", align_bytes=64) for t in range(PACK)]
         for tile in ure + uim + uimu:
             nc.gpsimd.memset(tile[:, S:], 0.0)
         ident = keep.tile([P, P], F32, name="ident", align_bytes=64)
@@ -129,14 +129,20 @@ def tile_picked_yacoust_log_p_kernel(
             nc.vector.tensor_scalar(ure[t][:, :S], product(0, t)[:], 2.5 * math.exp(SHIFT), None, ALU.mult)
         for t in range(PACK):
             nc.vector.tensor_copy(uim[t][:, :S], product(1, t)[:])
+            nc.gpsimd.tensor_scalar(uimu[t][:, :S], uim[t][:, :S], unit_t[:, t : t + 1], 0.0, ALU.mult, ALU.add)
         halves = range(U // BANK)
-        for t in range(PACK):
+
+        def inverses(t):
             nc.scalar.activation(inv_a[:, t, :], lnr[:, t, :], ACT.Sigmoid, scale=-1.0, bias=-SHIFT)
             nc.scalar.activation(lnr[:, t, :], lnr[:, t, :], ACT.Sigmoid, scale=-1.0)
+
+        for t in range(PACK - 1):
+            inverses(t)
 
         def piece(tile, h):
             return tile[:, BANK // 16 * h : BANK // 16 * (h + 1)]
 
+        ia_early = keep.tile([P, PACK, GROUP], F32, name="ia_early", align_bytes=64)
         amp = keep.tile([P, PACK, U], F32, name="amp", align_bytes=64)
         blocks = BANK // P
         for t in range(PACK):
@@ -146,24 +152,26 @@ def tile_picked_yacoust_log_p_kernel(
                 cols = slice(BANK * h, BANK * (h + 1))
                 ga = ring.tile([P, BANK], F32, name="ga", align_bytes=64, bufs=8)
                 gb = ring.tile([P, BANK], F32, name="gb", align_bytes=64, bufs=8)
-                nc.vector.tensor_tensor(ga[:], ure[t][:].indirect(piece(pa_t, h)), inv_a[:, t, cols], ALU.mult)
                 nc.vector.tensor_tensor(gb[:], uim[t][:].indirect(piece(pb_t, h)), lnr[:, t, cols], ALU.mult)
+                nc.vector.tensor_tensor(ga[:], ure[t][:].indirect(piece(pa_t, h)), inv_a[:, t, cols], ALU.mult)
                 both, alone = bank(2 * h), bank(2 * h + 1)
+                dst = slice(blocks * h, blocks * (h + 1))
                 for j in range(blocks):
                     blk = slice(P * j, P * (j + 1))
                     nc.tensor.transpose(alone[:, blk], gb[:, blk], ident[:])
-                for j in range(blocks):
-                    blk = slice(P * j, P * (j + 1))
-                    nc.tensor.matmul(both[:, blk], ga[:, blk], ident[:], start=True, stop=False, is_transpose=True)
-                    nc.tensor.matmul(both[:, blk], gb[:, blk], ident[:], start=False, stop=True, is_transpose=True)
-                dst = slice(blocks * h, blocks * (h + 1))
                 nc.scalar.activation(
                     sq_b[:, dst, :], alone[:].rearrange("p (j f) -> p j f", f=P), ACT.Square, scale=math.sqrt(3.36)
                 )
+                for j in range(blocks):
+                    blk = slice(P * j, P * (j + 1))
+                    nc.tensor.matmul(both[:, blk], gb[:, blk], ident[:], start=True, stop=False, is_transpose=True)
+                    nc.tensor.matmul(both[:, blk], ga[:, blk], ident[:], start=False, stop=True, is_transpose=True)
                 nc.scalar.activation(sq_sum[:, dst, :], both[:].rearrange("p (j f) -> p j f", f=P), ACT.Square, scale=0.8)
-            if t == 0:
-                for u in range(PACK):
-                    nc.vector.tensor_scalar(uimu[u][:, :S], uim[u][:, :S], unit_t[:, u : u + 1], None, ALU.mult)
+                if (t, h) == (0, 0):
+                    inverses(PACK - 1)
+                u = 2 * t + h - 3
+                if 0 <= u < 2:
+                    nc.scalar.activation(ia_early[:, u, :], uimu[u][:].indirect(pa_t[:, : GROUP // 16]), ACT.Copy)
             for h in range(2):
                 total = bank(4 + 2 * (t % 2) + h)
                 for j in range(blocks):
@@ -178,33 +186,39 @@ def tile_picked_yacoust_log_p_kernel(
                     bias=0.05,
                 )
 
-        ia_early = keep.tile([P, PACK, GROUP], F32, name="ia_early", align_bytes=64)
-        for t in range(PACK):
-            nc.scalar.activation(ia_early[:, t, :], uimu[t][:].indirect(pa_t[:, : GROUP // 16]), ACT.Copy)
         ia_late = keep.tile([P, PACK, U], F32, name="ia_late", tag="lnr", align_bytes=64)
-        for lo, hi in ((GROUP, BANK), (BANK, U)):
-            for t in range(PACK):
-                nc.vector.tensor_copy(ia_late[:, t, lo:hi], uimu[t][:].indirect(pa_t[:, lo // 16 : hi // 16]))
+        for t in range(2, PACK):
+            nc.vector.tensor_copy(ia_early[:, t, :], uimu[t][:].indirect(pa_t[:, : GROUP // 16]))
+        for t in range(PACK):
+            nc.vector.tensor_copy(ia_late[:, t, GROUP:], uimu[t][:].indirect(pa_t[:, GROUP // 16 :]))
 
+        lg = [keep.tile([P, PACK, GROUP], F32, name=f"lg{g}", align_bytes=64) for g in range(U // GROUP)]
         for g in range(U // GROUP):
-            cols = slice(GROUP * g, GROUP * (g + 1))
-            lg = ring.tile([P, PACK, GROUP], F32, name="lg", align_bytes=64, bufs=4)
-            nc.scalar.activation(lg[:], amp[:, :, cols], ACT.Ln, bias=0.2)
-            woven = ring.tile([P, GROUP, PACK], BF16, name="woven", align_bytes=64)
+            nc.scalar.activation(lg[g][:], amp[:, :, GROUP * g : GROUP * (g + 1)], ACT.Ln, bias=0.2)
+
+        spans = [(0, 256), (256, 512), (512, 768), (768, 896), (896, 1024)]
+        woven = {}
+
+        def weave(i):
+            lo, hi = spans[i]
+            woven[i] = ring.tile([P, hi - lo, PACK], BF16, name="woven", align_bytes=64, bufs=3)
             nc.vector.tensor_tensor(
-                woven[:].rearrange("p (c i) t -> p c t i", i=2),
-                (ia_early[:] if g == 0 else ia_late[:, :, cols]).rearrange("p t (c i) -> p c t i", i=2),
-                lg[:].rearrange("p t (c i) -> p c t i", i=2),
+                woven[i][:].rearrange("p (c i) t -> p c t i", i=2),
+                (ia_early[:] if i == 0 else ia_late[:, :, lo:hi]).rearrange("p t (c i) -> p c t i", i=2),
+                lg[lo // GROUP][:, :, lo % GROUP : lo % GROUP + hi - lo].rearrange("p t (c i) -> p c t i", i=2),
                 ALU.mult,
             )
-            codes = ring.tile([P, GROUP], U32, name="codes", align_bytes=64)
-            scales = ring.tile([P, GROUP], U8, name="scales", align_bytes=64)
+
+        def finish(i):
+            lo, hi = spans[i]
+            codes = ring.tile([P, hi - lo], U32, name="codes", align_bytes=64)
+            scales = ring.tile([P, hi - lo], U8, name="scales", align_bytes=64)
             nc.vector.quantize_mx(
-                out=codes[:].bitcast(FP8X4), scales=scales[:], in_=woven[:].rearrange("p n t -> p (n t)")
+                out=codes[:].bitcast(FP8X4), scales=scales[:], in_=woven[i][:].rearrange("p n t -> p (n t)")
             )
-            acc = bank(g)
+            acc = bank(i)
             nc.tensor.matmul_mx(
-                out=acc[:, :GROUP],
+                out=acc[:, : hi - lo],
                 lhsT=w3w[:].bitcast(FP4X4),
                 lhsT_scale=w3s[:],
                 rhs=codes[:].bitcast(FP8X4),
@@ -212,6 +226,12 @@ def tile_picked_yacoust_log_p_kernel(
                 start=True,
                 stop=True,
             )
-            res = ring.tile([P, GROUP], F32, name="res", align_bytes=64, bufs=4)
-            nc.scalar.copy(res[:], acc[:, :GROUP])
-            nc.sync.dma_start(out=out[:, cols], in_=res[:])
+            res = ring.tile([P, hi - lo], F32, name="res", align_bytes=64, bufs=5)
+            nc.scalar.copy(res[:], acc[:, : hi - lo])
+            (nc.scalar if hi == U else nc.sync).dma_start(out=out[:, lo:hi], in_=res[:])
+
+        weave(0)
+        for i in range(1, len(spans)):
+            weave(i)
+            finish(i - 1)
+        finish(len(spans) - 1)

@@ -19,16 +19,30 @@ ACT = mybir.ActivationFunctionType
 ALU = mybir.AluOpType
 
 P = 128
-PACK = 4
+SLABS = 4
 BANK = 512
+BLOCKS = BANK // P
+QUARTER = U // 4
+PER_COLUMN = 16
 SPARE = 16
-GROUP = 256
 SHIFT = 41.5
+SQUARES = 3.36
+CROSS = 0.8 / math.sqrt(SQUARES)
+REAL_SCALE = 2.5 * CROSS * math.exp(SHIFT)
+REAL_ON_VECTOR = 2
+IA_ON_SCALAR = QUARTER
+SPANS = ((0, 256), (256, 512), (512, 768), (768, 896), (896, 1024))
 
 
-def load_scale_rows(queue, tile, scales):
+def load_scale_rows(nc, tile, scales):
     for q in range(4):
-        queue.dma_start(out=tile[32 * q : 32 * q + 4, :].bitcast(I32), in_=scales[0, 4 * q : 4 * q + 4, :].bitcast(I32))
+        nc.sync.dma_start(
+            out=tile[32 * q : 32 * q + 4, :].bitcast(I32), in_=scales[0, 4 * q : 4 * q + 4, :].bitcast(I32)
+        )
+
+
+def entries(list_tile, lo, hi):
+    return list_tile[:, lo // PER_COLUMN : hi // PER_COLUMN]
 
 
 def tile_picked_yacoust_log_p_kernel(
@@ -43,195 +57,208 @@ def tile_picked_yacoust_log_p_kernel(
         def bank(b):
             return psum.tile([P, BANK], F32, name=f"bank{b}", tag=f"bank{b}")
 
-        offs_t = keep.tile([P, S // 16], U16, name="offs_t")
-        pa_t = keep.tile([P, U // 16], U16, name="pa_t")
-        pb_t = keep.tile([P, U // 16], U16, name="pb_t")
-        xw = keep.tile([P, T], I32, name="xw", align_bytes=64)
-        xs = keep.tile([P, T], U8, name="xs", align_bytes=64)
-        ww = [keep.tile([P, 2 * H], U8, name=f"ww{i}", align_bytes=64) for i in range(2)]
-        ws = [keep.tile([P, H], U8, name=f"ws{i}", align_bytes=64) for i in range(2)]
-        w3w = keep.tile([P, 2 * N], U8, name="w3w", align_bytes=64)
-        w3s = keep.tile([P, N], U8, name="w3s", align_bytes=64)
-        unit_t = keep.tile([P, PACK], F32, name="unit_t")
-        rad_t = [keep.tile([P, PACK, GROUP], F32, name=f"rad{g}", align_bytes=64) for g in range(U // GROUP)]
-        rad_rows = rad.rearrange("(p t) r -> p t r", t=PACK)
+        offs_t = keep.tile([P, S // PER_COLUMN], U16, name="offs_t")
+        pa_t = keep.tile([P, U // PER_COLUMN], U16, name="pa_t")
+        pb_t = keep.tile([P, U // PER_COLUMN], U16, name="pb_t")
+        x_w = keep.tile([P, T], I32, name="x_w", align_bytes=64)
+        x_s = keep.tile([P, T], U8, name="x_s", align_bytes=64)
+        w_w = [keep.tile([P, 2 * H], U8, name=f"w_w{i}", align_bytes=64) for i in range(2)]
+        w_s = [keep.tile([P, H], U8, name=f"w_s{i}", align_bytes=64) for i in range(2)]
+        w3_w = keep.tile([P, 2 * N], U8, name="w3_w", align_bytes=64)
+        w3_s = keep.tile([P, N], U8, name="w3_s", align_bytes=64)
+        unit_t = keep.tile([P, SLABS], F32, name="unit_t")
+        rad_t = [keep.tile([P, SLABS, QUARTER], F32, name=f"rad{g}", align_bytes=64) for g in range(4)]
+        rad_rows = rad.rearrange("(p t) r -> p t r", t=SLABS)
 
-        for tile in (xs, ws[0], ws[1], w3s):
+        def load_rad(queue, g):
+            queue.dma_start(out=rad_t[g][:], in_=rad_rows[:, :, QUARTER * g : QUARTER * (g + 1)])
+
+        for tile in (x_s, w_s[0], w_s[1], w3_s):
             nc.gpsimd.memset(tile[:].bitcast(I32), 0)
 
-        nc.sync.dma_start(out=xw[:], in_=x_words[0].rearrange("p n t -> p (n t)").bitcast(I32))
+        nc.sync.dma_start(out=x_w[:], in_=x_words[0].rearrange("p n t -> p (n t)").bitcast(I32))
         nc.sync.dma_start(offs_t[:], offs)
-        nc.scalar.dma_start(out=rad_t[0][:], in_=rad_rows[:, :, 0 * GROUP : 1 * GROUP])
-        nc.scalar.dma_start(out=rad_t[1][:], in_=rad_rows[:, :, 1 * GROUP : 2 * GROUP])
-        load_scale_rows(nc.sync, xs, x_scales)
-        nc.sync.dma_start(out=ww[0][:].bitcast(I32), in_=w1_words[0].bitcast(I32))
-        load_scale_rows(nc.sync, ws[0], w1_scales)
-        nc.sync.dma_start(out=rad_t[2][:], in_=rad_rows[:, :, 2 * GROUP : 3 * GROUP])
-        nc.sync.dma_start(out=rad_t[3][:], in_=rad_rows[:, :, 3 * GROUP : 4 * GROUP])
-        nc.sync.dma_start(out=ww[1][:].bitcast(I32), in_=w2_words[0].bitcast(I32))
-        load_scale_rows(nc.sync, ws[1], w2_scales)
-        nc.sync.dma_start(out=unit_t[:], in_=unit.rearrange("(p t) o -> p (t o)", t=PACK))
+        for g in range(3):
+            load_rad(nc.scalar, g)
+        load_scale_rows(nc, x_s, x_scales)
+        load_rad(nc.sync, 3)
+        for i, (words, scales) in enumerate(((w1_words, w1_scales), (w2_words, w2_scales))):
+            nc.sync.dma_start(out=w_w[i][:].bitcast(I32), in_=words[0].bitcast(I32))
+            load_scale_rows(nc, w_s[i], scales)
         nc.sync.dma_start(pa_t[:], pa)
         nc.sync.dma_start(pb_t[:], pb)
-        nc.sync.dma_start(out=w3w[:].bitcast(I32), in_=w3_words[0].bitcast(I32))
-        load_scale_rows(nc.sync, w3s, w3_scales)
+        nc.sync.dma_start(out=unit_t[:], in_=unit.rearrange("(p t) o -> p (t o)", t=SLABS))
+        nc.sync.dma_start(out=w3_w[:].bitcast(I32), in_=w3_words[0].bitcast(I32))
+        load_scale_rows(nc, w3_s, w3_scales)
 
-        ure = [keep.tile([P, S + SPARE], F32, name=f"ure{t}", align_bytes=64) for t in range(PACK)]
-        uim = [keep.tile([P, S + SPARE], F32, name=f"uim{t}", align_bytes=64) for t in range(PACK)]
-        uimu = [keep.tile([P, U - GROUP + SPARE], F32, name=f"uimu{t}", align_bytes=64) for t in range(PACK)]
-        for tile in ure + uim + uimu:
+        ure = [keep.tile([P, S + SPARE], F32, name=f"ure{t}", align_bytes=64) for t in range(SLABS)]
+        uim = [keep.tile([P, S + SPARE], F32, name=f"uim{t}", align_bytes=64) for t in range(SLABS)]
+        uim_unit = [
+            keep.tile([P, U - IA_ON_SCALAR + SPARE], F32, name=f"uim_unit{t}", align_bytes=64) for t in range(SLABS)
+        ]
+        for tile in ure + uim + uim_unit:
             nc.gpsimd.memset(tile[:, S:], 0.0)
         ident = keep.tile([P, P], F32, name="ident", align_bytes=64)
         make_identity(nc, ident[:])
 
-        xgw = keep.tile([P, S], U32, name="xgw", align_bytes=64)
-        xgs = keep.tile([P, S], U8, name="xgs", align_bytes=64)
-        wd = [keep.tile([P, 2 * H], U8, name=f"wd{i}", align_bytes=64) for i in range(2)]
-        wsd = [keep.tile([P, H], U8, name=f"wsd{i}", align_bytes=64) for i in range(2)]
-
-        def deal_words(i):
+        picked_w = keep.tile([P, S], U32, name="picked_w", align_bytes=64)
+        picked_s = keep.tile([P, S], U8, name="picked_s", align_bytes=64)
+        nc.vector.tensor_copy(picked_w[:], x_w[:].bitcast(U32).indirect(offs_t[:]))
+        nc.vector.tensor_copy(picked_s[:], x_s[:].indirect(offs_t[:]))
+        dealt_w = [keep.tile([P, 2 * H], U8, name=f"dealt_w{i}", align_bytes=64) for i in range(2)]
+        dealt_s = [keep.tile([P, H], U8, name=f"dealt_s{i}", align_bytes=64) for i in range(2)]
+        for i in range(2):
             nc.vector.tensor_copy(
-                out=wd[i][:].rearrange("p (t m b) -> p t m b", t=PACK, b=2),
-                in_=ww[i][:].rearrange("p (m t b) -> p t m b", t=PACK, b=2),
+                out=dealt_w[i][:].rearrange("p (t m b) -> p t m b", t=SLABS, b=2),
+                in_=w_w[i][:].rearrange("p (m t b) -> p t m b", t=SLABS, b=2),
             )
-
-        def deal_scales(i):
             nc.vector.tensor_copy(
-                out=wsd[i][:].rearrange("p (t m) -> p t m", t=PACK),
-                in_=ws[i][:].rearrange("p (m t) -> p t m", t=PACK),
+                out=dealt_s[i][:].rearrange("p (t m) -> p t m", t=SLABS),
+                in_=w_s[i][:].rearrange("p (m t) -> p t m", t=SLABS),
             )
-
-        nc.vector.tensor_copy(xgw[:], xw[:].bitcast(U32).indirect(offs_t[:]))
-        nc.vector.tensor_copy(xgs[:], xs[:].indirect(offs_t[:]))
-        deal_words(0)
-        deal_scales(0)
-        deal_words(1)
-        deal_scales(1)
 
         def product(i, t):
             acc = bank(2 * t + i)
             nc.tensor.matmul_mx(
                 out=acc[:],
-                lhsT=wd[i][:, 2 * P * t : 2 * P * (t + 1)].bitcast(FP4X4),
-                lhsT_scale=wsd[i][:, P * t : P * (t + 1)],
-                rhs=xgw[:].bitcast(FP8X4),
-                rhs_scale=xgs[:],
+                lhsT=dealt_w[i][:, 2 * P * t : 2 * P * (t + 1)].bitcast(FP4X4),
+                lhsT_scale=dealt_s[i][:, P * t : P * (t + 1)],
+                rhs=picked_w[:].bitcast(FP8X4),
+                rhs_scale=picked_s[:],
                 start=True,
                 stop=True,
             )
             return acc
 
-        lnr = keep.tile([P, PACK, U], F32, name="lnr", tag="lnr", align_bytes=64)
-        inv_a = keep.tile([P, PACK, U], F32, name="inv_a", align_bytes=64)
-        for g in range(U // GROUP):
-            nc.scalar.activation(lnr[:, :, GROUP * g : GROUP * (g + 1)], rad_t[g][:], ACT.Ln, scale=2.0)
-        for t in range(PACK):
-            nc.vector.tensor_scalar(ure[t][:, :S], product(0, t)[:], 2.5 * math.exp(SHIFT), None, ALU.mult)
-        for t in range(PACK):
-            nc.vector.tensor_copy(uim[t][:, :S], product(1, t)[:])
-            nc.gpsimd.tensor_scalar(uimu[t][:, :S], uim[t][:, :S], unit_t[:, t : t + 1], 0.0, ALU.mult, ALU.add)
-        halves = range(U // BANK)
+        inv_b = keep.tile([P, SLABS, U], F32, name="inv_b", align_bytes=64)
+        inv_a = keep.tile([P, SLABS, U], F32, name="inv_a", align_bytes=64)
+        for g in range(4):
+            nc.scalar.activation(inv_b[:, :, QUARTER * g : QUARTER * (g + 1)], rad_t[g][:], ACT.Ln, scale=2.0)
+        for t in range(SLABS):
+            real, imag = product(0, t), product(1, t)
+            if t < REAL_ON_VECTOR:
+                nc.vector.tensor_scalar(ure[t][:, :S], real[:], REAL_SCALE, None, ALU.mult)
+            else:
+                nc.scalar.activation(ure[t][:, :S], real[:], ACT.Copy, scale=REAL_SCALE)
+            nc.scalar.copy(uim[t][:, :S], imag[:])
+            nc.scalar.activation(inv_a[:, t, :], inv_b[:, t, :], ACT.Sigmoid, scale=-1.0, bias=-SHIFT)
+            nc.scalar.activation(inv_b[:, t, :], inv_b[:, t, :], ACT.Sigmoid, scale=-1.0)
 
-        def inverses(t):
-            nc.scalar.activation(inv_a[:, t, :], lnr[:, t, :], ACT.Sigmoid, scale=-1.0, bias=-SHIFT)
-            nc.scalar.activation(lnr[:, t, :], lnr[:, t, :], ACT.Sigmoid, scale=-1.0)
+        ia_first = keep.tile([P, SLABS, IA_ON_SCALAR], F32, name="ia_first", align_bytes=64)
+        amp = [keep.tile([P, 2, BLOCKS, P], F32, name=f"amp{t}", align_bytes=64) for t in range(SLABS)]
+        scaled_a = keep.tile([P, SLABS, U], F32, name="scaled_a", tag="a_then_ia", align_bytes=64)
+        back = {}
 
-        for t in range(PACK - 1):
-            inverses(t)
+        def turn_back(t, j):
+            if t == 0:
+                back[j] = bank(j)
+            nc.tensor.transpose(back[j][:, P * t : P * (t + 1)], amp[t][:, j % 2, j // 2, :], ident[:])
 
-        def piece(tile, h):
-            return tile[:, BANK // 16 * h : BANK // 16 * (h + 1)]
-
-        ia_early = keep.tile([P, PACK, GROUP], F32, name="ia_early", align_bytes=64)
-        amp = keep.tile([P, PACK, U], F32, name="amp", align_bytes=64)
-        blocks = BANK // P
-        for t in range(PACK):
-            sq_sum = ring.tile([P, U // P, P], F32, name="sq_sum", align_bytes=64)
-            sq_b = ring.tile([P, U // P, P], F32, name="sq_b", align_bytes=64)
-            for h in halves:
-                cols = slice(BANK * h, BANK * (h + 1))
-                ga = ring.tile([P, BANK], F32, name="ga", align_bytes=64, bufs=8)
-                gb = ring.tile([P, BANK], F32, name="gb", align_bytes=64, bufs=8)
-                nc.vector.tensor_tensor(gb[:], uim[t][:].indirect(piece(pb_t, h)), lnr[:, t, cols], ALU.mult)
-                nc.vector.tensor_tensor(ga[:], ure[t][:].indirect(piece(pa_t, h)), inv_a[:, t, cols], ALU.mult)
-                both, alone = bank(2 * h), bank(2 * h + 1)
-                dst = slice(blocks * h, blocks * (h + 1))
-                for j in range(blocks):
-                    blk = slice(P * j, P * (j + 1))
-                    nc.tensor.transpose(alone[:, blk], gb[:, blk], ident[:])
-                nc.scalar.activation(
-                    sq_b[:, dst, :], alone[:].rearrange("p (j f) -> p j f", f=P), ACT.Square, scale=math.sqrt(3.36)
-                )
-                for j in range(blocks):
-                    blk = slice(P * j, P * (j + 1))
-                    nc.tensor.matmul(both[:, blk], gb[:, blk], ident[:], start=True, stop=False, is_transpose=True)
-                    nc.tensor.matmul(both[:, blk], ga[:, blk], ident[:], start=False, stop=True, is_transpose=True)
-                nc.scalar.activation(sq_sum[:, dst, :], both[:].rearrange("p (j f) -> p j f", f=P), ACT.Square, scale=0.8)
-                if (t, h) == (0, 0):
-                    inverses(PACK - 1)
-                u = 2 * t + h - 3
-                if 0 <= u < 2:
-                    nc.scalar.activation(ia_early[:, u, :], uimu[u][:].indirect(pa_t[:, : GROUP // 16]), ACT.Copy)
+        for t in range(SLABS):
+            squares = []
             for h in range(2):
-                total = bank(4 + 2 * (t % 2) + h)
-                for j in range(blocks):
-                    blk = slice(P * j, P * (j + 1))
-                    src = 2 * j + h
-                    nc.tensor.matmul(total[:, blk], sq_b[:, src, :], ident[:], start=True, stop=False, is_transpose=True)
-                    nc.tensor.matmul(total[:, blk], sq_sum[:, src, :], ident[:], start=False, stop=True, is_transpose=True)
+                lo, hi = BANK * h, BANK * (h + 1)
+                pair = ring.tile([P, 2, BANK], F32, name="pair", align_bytes=64, bufs=2 * SLABS)
+                nc.vector.tensor_tensor(
+                    scaled_a[:, t, lo:hi], ure[t][:].indirect(entries(pa_t, lo, hi)), inv_a[:, t, lo:hi], ALU.mult
+                )
+                nc.vector.tensor_tensor(
+                    pair[:, 0, :], uim[t][:].indirect(entries(pb_t, lo, hi)), inv_b[:, t, lo:hi], ALU.mult
+                )
+                nc.vector.scalar_tensor_tensor(
+                    pair[:, 1, :], pair[:, 0, :], CROSS, scaled_a[:, t, lo:hi], ALU.mult, ALU.add
+                )
+                nc.scalar.activation(pair[:], pair[:], ACT.Square)
+                squares.append(pair)
+                step = 2 * t + h
+                if step == 1:
+                    for u in range(SLABS):
+                        nc.vector.tensor_scalar(uim_unit[u][:, :S], uim[u][:, :S], unit_t[:, u : u + 1], None, ALU.mult)
+                if 2 <= step < 2 + SLABS:
+                    nc.scalar.activation(
+                        ia_first[:, step - 2, :],
+                        uim_unit[step - 2][:].indirect(entries(pa_t, 0, IA_ON_SCALAR)),
+                        ACT.Copy,
+                    )
+            for e in range(2):
+                total = bank(BLOCKS + 2 * (t % 2) + e)
+                for n in range(BLOCKS):
+                    h, j = divmod(2 * n + e, BLOCKS)
+                    for term in range(2):
+                        nc.tensor.matmul(
+                            total[:, P * n : P * (n + 1)],
+                            squares[h][:, term, P * j : P * (j + 1)],
+                            ident[:],
+                            start=term == 0,
+                            stop=term == 1,
+                            is_transpose=True,
+                        )
                 nc.scalar.activation(
-                    amp[:, t, :].rearrange("p (j h r) -> p j h r", h=2, r=P)[:, :, h, :],
-                    total[:].rearrange("p (j r) -> p j r", r=P),
+                    amp[t][:, e, :, :],
+                    total[:].rearrange("p (n m) -> p n m", m=P),
                     ACT.Sqrt,
                     bias=0.05,
+                    scale=SQUARES,
                 )
+            for j in range(BLOCKS):
+                turn_back(t, j)
+        for j in range(BLOCKS, 2 * BLOCKS):
+            for t in range(SLABS):
+                turn_back(t, j)
 
-        ia_late = keep.tile([P, PACK, U], F32, name="ia_late", tag="lnr", align_bytes=64)
-        for t in range(2, PACK):
-            nc.vector.tensor_copy(ia_early[:, t, :], uimu[t][:].indirect(pa_t[:, : GROUP // 16]))
-        for t in range(PACK):
-            nc.vector.tensor_copy(ia_late[:, t, GROUP:], uimu[t][:].indirect(pa_t[:, GROUP // 16 :]))
+        ia_rest = keep.tile([P, SLABS, U], F32, name="ia_rest", tag="a_then_ia", align_bytes=64)
+        for t in range(SLABS):
+            nc.vector.tensor_copy(
+                ia_rest[:, t, IA_ON_SCALAR:], uim_unit[t][:].indirect(entries(pa_t, IA_ON_SCALAR, U))
+            )
 
-        lg = [keep.tile([P, PACK, GROUP], F32, name=f"lg{g}", align_bytes=64) for g in range(U // GROUP)]
-        for g in range(U // GROUP):
-            nc.scalar.activation(lg[g][:], amp[:, :, GROUP * g : GROUP * (g + 1)], ACT.Ln, bias=0.2)
+        logs = [keep.tile([P, SLABS, QUARTER], F32, name=f"logs{g}", align_bytes=64) for g in range(4)]
+        for j in range(2 * BLOCKS):
+            nc.scalar.activation(
+                logs[j // 2][:, :, P * (j % 2) : P * (j % 2 + 1)],
+                back[j][:].rearrange("p (t r) -> p t r", r=P),
+                ACT.Ln,
+                bias=0.2,
+            )
 
-        spans = [(0, 256), (256, 512), (512, 768), (768, 896), (896, 1024)]
         woven = {}
 
         def weave(i):
-            lo, hi = spans[i]
-            woven[i] = ring.tile([P, hi - lo, PACK], BF16, name="woven", align_bytes=64, bufs=3)
+            lo, hi = SPANS[i]
+            ia = ia_first if hi <= IA_ON_SCALAR else ia_rest
+            start = lo % QUARTER
+            woven[i] = ring.tile([P, hi - lo, SLABS], BF16, name="woven", align_bytes=64, bufs=3)
             nc.vector.tensor_tensor(
-                woven[i][:].rearrange("p (c i) t -> p c t i", i=2),
-                (ia_early[:] if i == 0 else ia_late[:, :, lo:hi]).rearrange("p t (c i) -> p c t i", i=2),
-                lg[lo // GROUP][:, :, lo % GROUP : lo % GROUP + hi - lo].rearrange("p t (c i) -> p c t i", i=2),
+                woven[i][:].rearrange("p (c r) t -> p c t r", r=2),
+                ia[:, :, lo:hi].rearrange("p t (c r) -> p c t r", r=2),
+                logs[lo // QUARTER][:, :, start : start + hi - lo].rearrange("p t (c r) -> p c t r", r=2),
                 ALU.mult,
             )
 
         def finish(i):
-            lo, hi = spans[i]
+            lo, hi = SPANS[i]
             codes = ring.tile([P, hi - lo], U32, name="codes", align_bytes=64)
             scales = ring.tile([P, hi - lo], U8, name="scales", align_bytes=64)
             nc.vector.quantize_mx(
-                out=codes[:].bitcast(FP8X4), scales=scales[:], in_=woven[i][:].rearrange("p n t -> p (n t)")
+                out=codes[:].bitcast(FP8X4), scales=scales[:], in_=woven[i][:].rearrange("p r t -> p (r t)")
             )
             acc = bank(i)
             nc.tensor.matmul_mx(
                 out=acc[:, : hi - lo],
-                lhsT=w3w[:].bitcast(FP4X4),
-                lhsT_scale=w3s[:],
+                lhsT=w3_w[:].bitcast(FP4X4),
+                lhsT_scale=w3_s[:],
                 rhs=codes[:].bitcast(FP8X4),
                 rhs_scale=scales[:],
                 start=True,
                 stop=True,
             )
-            res = ring.tile([P, hi - lo], F32, name="res", align_bytes=64, bufs=5)
-            nc.scalar.copy(res[:], acc[:, : hi - lo])
-            (nc.scalar if hi == U else nc.sync).dma_start(out=out[:, lo:hi], in_=res[:])
+            result = ring.tile([P, hi - lo], F32, name="result", align_bytes=64, bufs=len(SPANS))
+            nc.scalar.copy(result[:], acc[:, : hi - lo])
+            queue = nc.scalar if hi == U else nc.sync
+            queue.dma_start(out=out[:, lo:hi], in_=result[:])
 
         weave(0)
-        for i in range(1, len(spans)):
+        for i in range(1, len(SPANS)):
             weave(i)
             finish(i - 1)
-        finish(len(spans) - 1)
+        finish(len(SPANS) - 1)

import math
from contextlib import ExitStack

import concourse.mybir as mybir
from concourse.masks import make_identity

K, T, S, N, H, U = 512, 1024, 512, 128, 512, 1024
FLOPS = 2 * K * S * H * 2 + 2 * H * U * N

F32 = mybir.dt.float32
BF16 = mybir.dt.bfloat16
I32 = mybir.dt.int32
U32 = mybir.dt.uint32
U16 = mybir.dt.uint16
U8 = mybir.dt.uint8
FP8X4 = mybir.dt.float8_e4m3fn_x4
FP4X4 = mybir.dt.float4_e2m1fn_x4
ACT = mybir.ActivationFunctionType
ALU = mybir.AluOpType

P = 128
SLABS = 4
BANK = 512
BLOCKS = BANK // P
QUARTER = U // 4
PER_COLUMN = 16
SPARE = 16
SHIFT = 41.5
SQUARES = 3.36
CROSS = 0.8 / math.sqrt(SQUARES)
REAL_SCALE = 2.5 * CROSS * math.exp(SHIFT)
REAL_ON_VECTOR = 2
IA_ON_SCALAR = QUARTER
SPANS = ((0, 256), (256, 512), (512, 768), (768, 896), (896, 1024))


def load_scale_rows(nc, tile, scales):
    for q in range(4):
        nc.sync.dma_start(
            out=tile[32 * q : 32 * q + 4, :].bitcast(I32), in_=scales[0, 4 * q : 4 * q + 4, :].bitcast(I32)
        )


def entries(list_tile, lo, hi):
    return list_tile[:, lo // PER_COLUMN : hi // PER_COLUMN]


def tile_picked_yacoust_log_p_kernel(
    tc, x_words, x_scales, w1_words, w1_scales, w2_words, w2_scales, rad, unit, w3_words, w3_scales, offs, pa, pb, out
):
    nc = tc.nc
    with ExitStack() as ctx:
        keep = ctx.enter_context(tc.tile_pool(name="keep", bufs=1))
        ring = ctx.enter_context(tc.tile_pool(name="ring", bufs=2))
        psum = ctx.enter_context(tc.psum_pool(name="psum", bufs=1))

        def bank(b):
            return psum.tile([P, BANK], F32, name=f"bank{b}", tag=f"bank{b}")

        offs_t = keep.tile([P, S // PER_COLUMN], U16, name="offs_t")
        pa_t = keep.tile([P, U // PER_COLUMN], U16, name="pa_t")
        pb_t = keep.tile([P, U // PER_COLUMN], U16, name="pb_t")
        x_w = keep.tile([P, T], I32, name="x_w", align_bytes=64)
        x_s = keep.tile([P, T], U8, name="x_s", align_bytes=64)
        w_w = [keep.tile([P, 2 * H], U8, name=f"w_w{i}", align_bytes=64) for i in range(2)]
        w_s = [keep.tile([P, H], U8, name=f"w_s{i}", align_bytes=64) for i in range(2)]
        w3_w = keep.tile([P, 2 * N], U8, name="w3_w", align_bytes=64)
        w3_s = keep.tile([P, N], U8, name="w3_s", align_bytes=64)
        unit_t = keep.tile([P, SLABS], F32, name="unit_t")
        rad_t = [keep.tile([P, SLABS, QUARTER], F32, name=f"rad{g}", align_bytes=64) for g in range(4)]
        rad_rows = rad.rearrange("(p t) r -> p t r", t=SLABS)

        def load_rad(queue, g):
            queue.dma_start(out=rad_t[g][:], in_=rad_rows[:, :, QUARTER * g : QUARTER * (g + 1)])

        for tile in (x_s, w_s[0], w_s[1], w3_s):
            nc.gpsimd.memset(tile[:].bitcast(I32), 0)

        nc.sync.dma_start(out=x_w[:], in_=x_words[0].rearrange("p n t -> p (n t)").bitcast(I32))
        nc.sync.dma_start(offs_t[:], offs)
        for g in range(3):
            load_rad(nc.scalar, g)
        load_scale_rows(nc, x_s, x_scales)
        load_rad(nc.sync, 3)
        for i, (words, scales) in enumerate(((w1_words, w1_scales), (w2_words, w2_scales))):
            nc.sync.dma_start(out=w_w[i][:].bitcast(I32), in_=words[0].bitcast(I32))
            load_scale_rows(nc, w_s[i], scales)
        nc.sync.dma_start(pa_t[:], pa)
        nc.sync.dma_start(pb_t[:], pb)
        nc.sync.dma_start(out=unit_t[:], in_=unit.rearrange("(p t) o -> p (t o)", t=SLABS))
        nc.sync.dma_start(out=w3_w[:].bitcast(I32), in_=w3_words[0].bitcast(I32))
        load_scale_rows(nc, w3_s, w3_scales)

        ure = [keep.tile([P, S + SPARE], F32, name=f"ure{t}", align_bytes=64) for t in range(SLABS)]
        uim = [keep.tile([P, S + SPARE], F32, name=f"uim{t}", align_bytes=64) for t in range(SLABS)]
        uim_unit = [
            keep.tile([P, U - IA_ON_SCALAR + SPARE], F32, name=f"uim_unit{t}", align_bytes=64) for t in range(SLABS)
        ]
        for tile in ure + uim + uim_unit:
            nc.gpsimd.memset(tile[:, S:], 0.0)
        ident = keep.tile([P, P], F32, name="ident", align_bytes=64)
        make_identity(nc, ident[:])

        picked_w = keep.tile([P, S], U32, name="picked_w", align_bytes=64)
        picked_s = keep.tile([P, S], U8, name="picked_s", align_bytes=64)
        nc.vector.tensor_copy(picked_w[:], x_w[:].bitcast(U32).indirect(offs_t[:]))
        nc.vector.tensor_copy(picked_s[:], x_s[:].indirect(offs_t[:]))
        dealt_w = [keep.tile([P, 2 * H], U8, name=f"dealt_w{i}", align_bytes=64) for i in range(2)]
        dealt_s = [keep.tile([P, H], U8, name=f"dealt_s{i}", align_bytes=64) for i in range(2)]
        for i in range(2):
            nc.vector.tensor_copy(
                out=dealt_w[i][:].rearrange("p (t m b) -> p t m b", t=SLABS, b=2),
                in_=w_w[i][:].rearrange("p (m t b) -> p t m b", t=SLABS, b=2),
            )
            nc.vector.tensor_copy(
                out=dealt_s[i][:].rearrange("p (t m) -> p t m", t=SLABS),
                in_=w_s[i][:].rearrange("p (m t) -> p t m", t=SLABS),
            )

        def product(i, t):
            acc = bank(2 * t + i)
            nc.tensor.matmul_mx(
                out=acc[:],
                lhsT=dealt_w[i][:, 2 * P * t : 2 * P * (t + 1)].bitcast(FP4X4),
                lhsT_scale=dealt_s[i][:, P * t : P * (t + 1)],
                rhs=picked_w[:].bitcast(FP8X4),
                rhs_scale=picked_s[:],
                start=True,
                stop=True,
            )
            return acc

        inv_b = keep.tile([P, SLABS, U], F32, name="inv_b", align_bytes=64)
        inv_a = keep.tile([P, SLABS, U], F32, name="inv_a", align_bytes=64)
        for g in range(4):
            nc.scalar.activation(inv_b[:, :, QUARTER * g : QUARTER * (g + 1)], rad_t[g][:], ACT.Ln, scale=2.0)
        for t in range(SLABS):
            real, imag = product(0, t), product(1, t)
            if t < REAL_ON_VECTOR:
                nc.vector.tensor_scalar(ure[t][:, :S], real[:], REAL_SCALE, None, ALU.mult)
            else:
                nc.scalar.activation(ure[t][:, :S], real[:], ACT.Copy, scale=REAL_SCALE)
            nc.scalar.copy(uim[t][:, :S], imag[:])
            nc.scalar.activation(inv_a[:, t, :], inv_b[:, t, :], ACT.Sigmoid, scale=-1.0, bias=-SHIFT)
            nc.scalar.activation(inv_b[:, t, :], inv_b[:, t, :], ACT.Sigmoid, scale=-1.0)

        ia_first = keep.tile([P, SLABS, IA_ON_SCALAR], F32, name="ia_first", align_bytes=64)
        amp = [keep.tile([P, 2, BLOCKS, P], F32, name=f"amp{t}", align_bytes=64) for t in range(SLABS)]
        scaled_a = keep.tile([P, SLABS, U], F32, name="scaled_a", tag="a_then_ia", align_bytes=64)
        back = {}

        def turn_back(t, j):
            if t == 0:
                back[j] = bank(j)
            nc.tensor.transpose(back[j][:, P * t : P * (t + 1)], amp[t][:, j % 2, j // 2, :], ident[:])

        for t in range(SLABS):
            squares = []
            for h in range(2):
                lo, hi = BANK * h, BANK * (h + 1)
                pair = ring.tile([P, 2, BANK], F32, name="pair", align_bytes=64, bufs=2 * SLABS)
                nc.vector.tensor_tensor(
                    scaled_a[:, t, lo:hi], ure[t][:].indirect(entries(pa_t, lo, hi)), inv_a[:, t, lo:hi], ALU.mult
                )
                nc.vector.tensor_tensor(
                    pair[:, 0, :], uim[t][:].indirect(entries(pb_t, lo, hi)), inv_b[:, t, lo:hi], ALU.mult
                )
                nc.vector.scalar_tensor_tensor(
                    pair[:, 1, :], pair[:, 0, :], CROSS, scaled_a[:, t, lo:hi], ALU.mult, ALU.add
                )
                nc.scalar.activation(pair[:], pair[:], ACT.Square)
                squares.append(pair)
                step = 2 * t + h
                if step == 1:
                    for u in range(SLABS):
                        nc.vector.tensor_scalar(uim_unit[u][:, :S], uim[u][:, :S], unit_t[:, u : u + 1], None, ALU.mult)
                if 2 <= step < 2 + SLABS:
                    nc.scalar.activation(
                        ia_first[:, step - 2, :],
                        uim_unit[step - 2][:].indirect(entries(pa_t, 0, IA_ON_SCALAR)),
                        ACT.Copy,
                    )
            for e in range(2):
                total = bank(BLOCKS + 2 * (t % 2) + e)
                for n in range(BLOCKS):
                    h, j = divmod(2 * n + e, BLOCKS)
                    for term in range(2):
                        nc.tensor.matmul(
                            total[:, P * n : P * (n + 1)],
                            squares[h][:, term, P * j : P * (j + 1)],
                            ident[:],
                            start=term == 0,
                            stop=term == 1,
                            is_transpose=True,
                        )
                nc.scalar.activation(
                    amp[t][:, e, :, :],
                    total[:].rearrange("p (n m) -> p n m", m=P),
                    ACT.Sqrt,
                    bias=0.05,
                    scale=SQUARES,
                )
            for j in range(BLOCKS):
                turn_back(t, j)
        for j in range(BLOCKS, 2 * BLOCKS):
            for t in range(SLABS):
                turn_back(t, j)

        ia_rest = keep.tile([P, SLABS, U], F32, name="ia_rest", tag="a_then_ia", align_bytes=64)
        for t in range(SLABS):
            nc.vector.tensor_copy(
                ia_rest[:, t, IA_ON_SCALAR:], uim_unit[t][:].indirect(entries(pa_t, IA_ON_SCALAR, U))
            )

        logs = [keep.tile([P, SLABS, QUARTER], F32, name=f"logs{g}", align_bytes=64) for g in range(4)]
        for j in range(2 * BLOCKS):
            nc.scalar.activation(
                logs[j // 2][:, :, P * (j % 2) : P * (j % 2 + 1)],
                back[j][:].rearrange("p (t r) -> p t r", r=P),
                ACT.Ln,
                bias=0.2,
            )

        woven = {}

        def weave(i):
            lo, hi = SPANS[i]
            ia = ia_first if hi <= IA_ON_SCALAR else ia_rest
            start = lo % QUARTER
            woven[i] = ring.tile([P, hi - lo, SLABS], BF16, name="woven", align_bytes=64, bufs=3)
            nc.vector.tensor_tensor(
                woven[i][:].rearrange("p (c r) t -> p c t r", r=2),
                ia[:, :, lo:hi].rearrange("p t (c r) -> p c t r", r=2),
                logs[lo // QUARTER][:, :, start : start + hi - lo].rearrange("p t (c r) -> p c t r", r=2),
                ALU.mult,
            )

        def finish(i):
            lo, hi = SPANS[i]
            codes = ring.tile([P, hi - lo], U32, name="codes", align_bytes=64)
            scales = ring.tile([P, hi - lo], U8, name="scales", align_bytes=64)
            nc.vector.quantize_mx(
                out=codes[:].bitcast(FP8X4), scales=scales[:], in_=woven[i][:].rearrange("p r t -> p (r t)")
            )
            acc = bank(i)
            nc.tensor.matmul_mx(
                out=acc[:, : hi - lo],
                lhsT=w3_w[:].bitcast(FP4X4),
                lhsT_scale=w3_s[:],
                rhs=codes[:].bitcast(FP8X4),
                rhs_scale=scales[:],
                start=True,
                stop=True,
            )
            result = ring.tile([P, hi - lo], F32, name="result", align_bytes=64, bufs=len(SPANS))
            nc.scalar.copy(result[:], acc[:, : hi - lo])
            queue = nc.scalar if hi == U else nc.sync
            queue.dma_start(out=out[:, lo:hi], in_=result[:])

        weave(0)
        for i in range(1, len(SPANS)):
            weave(i)
            finish(i - 1)
        finish(len(SPANS) - 1)
